import numpy as np
import ml_dtypes


def mxq(x, axis, fmt="e4m3"):
    dtype, down = {"e4m3": (ml_dtypes.float8_e4m3fn, 7), "e5m2": (ml_dtypes.float8_e5m2, 14)}[fmt]
    v = np.moveaxis(np.asarray(x, np.float32).astype(ml_dtypes.bfloat16).astype(np.float64), axis, -1)
    blocks = v.reshape(v.shape[:-1] + (-1, 32))
    amax = np.abs(blocks).max(-1, keepdims=True)
    byte = np.maximum(np.where(amax > 0, np.frexp(amax)[1] - 1 + 127, 0) - down, 1)
    scale = np.exp2(byte - 127.0)
    codes = (blocks / scale).astype(np.float32).astype(dtype).astype(np.float64)
    return np.moveaxis((codes * scale).reshape(v.shape), -1, axis)


WIDE = False


def mx_kscale(k):
    if not WIDE:
        return np.ones(k)
    levels = np.array([10, -10, 5, -5, 0])
    if k % 512:
        return np.exp2(np.random.permutation(np.resize(levels, k // 32))).repeat(32)
    a = np.empty((k // 512, 16))
    for p in range(k // 512):
        a[p, :8] = np.random.permutation(np.resize(levels, 8))
        for g in range(8):
            far = levels[np.abs(levels - a[p, g]) >= 10]
            a[p, g + 8] = far[np.random.randint(len(far))]
    return np.exp2(a.ravel()).repeat(32)


BF16 = ml_dtypes.bfloat16


def bf(x):
    return np.asarray(x, np.float32).astype(BF16)


def f64(x):
    return np.asarray(x).astype(np.float64)


E2M1 = np.array([0.0, 0.5, 1.0, 1.5, 2.0, 3.0, 4.0, 6.0, -0.0, -0.5, -1.0, -1.5, -2.0, -3.0, -4.0, -6.0])


def pack_weight(w, fmt):
    k, n = w.shape
    w = f64(bf(w)).reshape(k // 32, 32, n)
    amax = np.abs(w).max(1)
    if fmt == "e4m3":
        byte = np.frexp(amax)[1] - 1 + 127 - 7
    else:
        mant, ex = np.frexp(amax / 6.0)
        byte = np.where(mant > 0.5, ex, ex - 1) + 127
    byte = np.clip(np.where(amax > 0, byte, 1), 1, 254)
    scaled = (w * np.exp2(127.0 - byte)[:, None, :]).reshape(k, n).astype(np.float32)
    by_word = np.ascontiguousarray(scaled.reshape(k // 512, 128, 4, n).transpose(0, 1, 3, 2))
    if fmt == "e4m3":
        words = by_word.astype(ml_dtypes.float8_e4m3fn).view(np.uint8)
    else:
        c = by_word.astype(ml_dtypes.float4_e2m1fn).view(np.uint8) & 0xF
        words = c[..., 0::2] | (c[..., 1::2] << 4)
    return np.ascontiguousarray(words), np.ascontiguousarray(byte.astype(np.uint8).reshape(k // 512, 16, n))


def unpack_weight(words, scales, fmt):
    g, p, n, _ = words.shape
    if fmt == "e4m3":
        vals = np.ascontiguousarray(words).view(ml_dtypes.float8_e4m3fn).astype(np.float64)
    else:
        nib = np.empty((g, p, n, 4), np.uint8)
        nib[..., 0::2] = words & 0xF
        nib[..., 1::2] = words >> 4
        vals = E2M1[nib]
    vals = vals * np.repeat(np.exp2(scales.astype(np.float64) - 127.0), 8, axis=1)[..., None]
    return vals.transpose(0, 1, 3, 2).reshape(g * 512, n)
def pack4(w):
    words, scales = pack_weight(w, "e2m1")
    return words.reshape(words.shape[0], 128, -1), scales


def unpack4(words, scales):
    return unpack_weight(words.reshape(words.shape[0], 128, -1, 2), scales, "e2m1")


E4M3FN = np.array([(-1.0 if i & 128 else 1.0) * ((1.0 + (i & 7) / 8.0) * 2.0 ** (((i >> 3) & 15) - 7) if i & 120 else (i & 7) * 2.0 ** -9) for i in range(256)])


def e4m3fn_bytes(y):
    return np.clip(np.asarray(y, np.float64), -448.0, 448.0).astype(np.float32).astype(ml_dtypes.float8_e4m3fn).view(np.uint8)


def e4m3fn_values(b):
    return E4M3FN[b]


A, O, V, B = 1536, 512, 1024, 128


def setup_inputs():
    s, u = mx_kscale(A), mx_kscale(A)
    orb = np.linalg.qr(np.random.standard_normal((A, A)))[0]
    Co, Cv = orb[:, :O].T / u, orb[:, O:]
    G = np.random.standard_normal((A, A))
    G = (G + G.T) / np.sqrt(2) * s * u[:, None]
    v = 0.5 * np.sqrt(A) * np.random.standard_normal((A, 1))
    G_scale = (np.abs(G).reshape(A, A // B, B).max(2) / 448).astype(np.float32)
    Co_scale = (np.abs(Co).reshape(O // B, B, A // B, B).max((1, 3)) / 448).astype(np.float32)
    Cv_words, Cv_scales = pack4(Cv / s[:, None])
    return {"G_bytes": e4m3fn_bytes(G / np.repeat(f64(G_scale), B, 1)),
            "G_scale": G_scale,
            "Cv_words": Cv_words,
            "Cv_scales": Cv_scales,
            "L": bf(v * Cv * u[:, None]),
            "Co_bytes": e4m3fn_bytes(Co / np.repeat(np.repeat(f64(Co_scale), B, 0), B, 1)),
            "Co_scale": Co_scale,
            "e_o": bf(-0.5 - 1.5 * np.random.random(O)),
            "e_v": bf(0.3 + 1.5 * np.random.random(V))}


def reference(G_bytes, G_scale, Cv_words, Cv_scales, L, Co_bytes, Co_scale, e_o, e_v):
    G = e4m3fn_values(G_bytes) * np.repeat(f64(G_scale), B, 1)
    Co = e4m3fn_values(Co_bytes) * np.repeat(np.repeat(f64(Co_scale), B, 0), B, 1)
    h = (mxq(G, 1, "e4m3") @ unpack4(Cv_words, Cv_scales)) + f64(L)
    f_ov = mxq(Co, 1, "e4m3") @ mxq(h, 0, "e4m3")
    mix = f_ov / (f64(e_o)[:, None] - f64(e_v)[None, :])
    return f_ov, mix

@@ -1,0 +1,287 @@
+from contextlib import ExitStack
+
+import concourse.mybir as mybir
+from concourse.masks import make_identity
+
+FLOPS = 2 * 1536 * 1536 * 1024 + 2 * 512 * 1536 * 1024
+
+A, O, V = 1536, 512, 1024
+P = 128
+
+F32 = mybir.dt.float32
+BF16 = mybir.dt.bfloat16
+I32 = mybir.dt.int32
+U32 = mybir.dt.uint32
+U8 = mybir.dt.uint8
+FP8 = mybir.dt.float8_e4m3fn
+FP8X4 = mybir.dt.float8_e4m3fn_x4
+FP4X4 = mybir.dt.float4_e2m1fn_x4
+MULT = mybir.AluOpType.mult
+ADD = mybir.AluOpType.add
+ACT = mybir.ActivationFunctionType
+
+NG = 3
+AHEAD = 5
+QLAG = 1
+QFIRST = True
+TOFF = 2
+MOFF = 1
+RB = 0
+LN0 = 18
+ADDS = [(1, "a", 0), (2, "a", 1), (2, "a", 2), (3, "a", 3), (3, "q", 0), (4, "q", 1)]
+ON_VECTOR = [u % 2 == 0 for u in range(24)]
+
+
+def tile_fock_orbital_transform_d6_kernel(
+    tc, G_bytes, G_scale, Cv_words, Cv_scales, L, Co_bytes, Co_scale, e_o, e_v, out_0, out_1
+):
+    nc = tc.nc
+    with ExitStack() as ctx:
+        keep = ctx.enter_context(tc.tile_pool(name="keep", bufs=1))
+        work = ctx.enter_context(tc.tile_pool(name="work", bufs=3))
+        psum = ctx.enter_context(tc.psum_pool(name="psum", bufs=4))
+        ctx.enter_context(tc.manual_schedule())
+
+        ident = keep.tile([P, P], F32, name="ident")
+        gs = keep.tile([P, NG, 4, 12], F32, name="gs")
+        cos = keep.tile([P, 12], F32, name="cos")
+        gb = [keep.tile([P, 2, A], U8, name=f"gb{j}", align_bytes=64) for j in range(6)]
+        cb = [keep.tile([P, 2, A], U8, name=f"cb{j}", align_bytes=64) for j in range(2)]
+        words = [keep.tile([P, NG, 1024], U8, name=f"words{v}", align_bytes=64) for v in range(2)]
+        cvs = keep.tile([P, NG, V], U8, name="cvs", align_bytes=64)
+        lt = [[keep.tile([P, 4, 512], BF16, name=f"lt{h}_{v}", align_bytes=64) for v in range(2)] for h in range(NG)]
+        eo = keep.tile([P, 4], BF16, name="eo")
+        ev = keep.tile([P, V], BF16, name="ev")
+        codes = [keep.tile([P, NG, 256], U32, name=f"codes{j}", align_bytes=64) for j in range(8)]
+        scales = [keep.tile([P, NG, 256], U8, name=f"scales{j}", align_bytes=64) for j in range(8)]
+        hc = [keep.tile([P, NG, 512], U32, name=f"hc{v}", align_bytes=64) for v in range(2)]
+        hs = [keep.tile([P, NG, 512], U8, name=f"hs{v}", align_bytes=64) for v in range(2)]
+        rec = [keep.tile([P, V], F32, name=f"rec{r}") for r in range(4)]
+        neo = keep.tile([P, 4], F32, name="neo")
+        dummy = keep.tile([P, 1], F32, name="dummy")
+
+        gv = G_bytes.rearrange("(h p t) k -> h p t k", p=P, t=4)
+        cv = Co_bytes.rearrange("(p r) k -> p r k", r=4)
+        lv = L.rearrange("(h p t) n -> h p t n", p=P, t=4)
+        wv = Cv_words.bitcast(I32).rearrange("g p w -> p g w")
+        sv = Cv_scales.bitcast(I32).rearrange("g q w -> q g w")
+        fv = out_0.rearrange("(p r) n -> p r n", r=4)
+        mv = out_1.rearrange("(p r) n -> p r n", r=4)
+
+        nc.vector.memset(dummy[:], 1.0)
+        nc.gpsimd.memset(cvs[:].bitcast(I32), 0)
+        make_identity(nc, ident[:])
+        nc.scalar.dma_start(out=gs[:], in_=G_scale.rearrange("(h p t) b -> p h t b", p=P, t=4))
+        nc.scalar.activation(out=dummy[:], in_=dummy[:], func=ACT.Ln)
+        nc.sync.dma_start(out=gb[0][:, 0, :], in_=gv[0][:, 0, :])
+        nc.sync.dma_start(out=gb[0][:, 1, :], in_=gv[0][:, 1, :])
+        for q in range(4):
+            nc.scalar.dma_start(
+                out=cvs[:].bitcast(I32)[32 * q : 32 * q + 4], in_=sv[4 * q : 4 * q + 4]
+            )
+        nc.sync.dma_start(out=gb[1][:], in_=gv[0][:, 2:4, :])
+        nc.sync.dma_start(out=words[0][:].bitcast(I32), in_=wv[:, :, 0:256])
+        nc.sync.dma_start(out=gb[2][:], in_=gv[1][:, 0:2, :])
+        nc.sync.dma_start(out=lt[0][0][:], in_=lv[0][:, :, 0:512])
+        nc.sync.dma_start(out=gb[3][:], in_=gv[1][:, 2:4, :])
+        nc.sync.dma_start(out=gb[4][:], in_=gv[2][:, 0:2, :])
+        nc.sync.dma_start(out=lt[1][0][:], in_=lv[1][:, :, 0:512])
+        nc.sync.dma_start(out=gb[5][:], in_=gv[2][:, 2:4, :])
+        for c in range(4):
+            nc.sync.dma_start(out=cos[32 * c : 32 * c + 32], in_=Co_scale[c].partition_broadcast(32))
+        nc.sync.dma_start(out=cb[0][:], in_=cv[:, 0:2, :])
+        nc.sync.dma_start(out=lt[2][0][:], in_=lv[2][:, :, 0:512])
+        nc.sync.dma_start(out=cb[1][:], in_=cv[:, 2:4, :])
+        nc.sync.dma_start(out=words[1][:].bitcast(I32), in_=wv[:, :, 256:512])
+        nc.sync.dma_start(out=eo[:], in_=e_o.rearrange("(p r) -> p r", r=4))
+        for h in range(NG):
+            nc.sync.dma_start(out=lt[h][1][:], in_=lv[h][:, :, 512:1024])
+        nc.sync.dma_start(out=ev[:], in_=e_v.partition_broadcast(P))
+
+        wide = {}
+        tps = {}
+        grouped = {}
+        hb = {}
+        hi = {}
+
+        def widen(u):
+            j, g = u // 3, u % 3
+            w = work.tile([P, 2, 512], BF16, name="wide", bufs=8, align_bytes=64)
+            wide[u] = w
+            for q in range(4):
+                b = 4 * g + q
+                for a in range(2):
+                    src = (gb[j] if j < 6 else cb[j - 6])[:, a, 128 * b : 128 * b + 128].bitcast(FP8)
+                    sc = gs[:, j // 2, 2 * (j % 2) + a, b : b + 1] if j < 6 else cos[:, b : b + 1]
+                    if ON_VECTOR[u]:
+                        nc.vector.tensor_scalar(
+                            out=w[:, a, :].rearrange("p (u x e) -> p x u e", u=2, e=2)[:, 32 * q : 32 * q + 32],
+                            in0=src.rearrange("p (x u e) -> p x u e", u=2, e=2),
+                            scalar1=sc,
+                            scalar2=None,
+                            op0=MULT,
+                        )
+                    else:
+                        nc.scalar.activation(out=w[:, a, 128 * q : 128 * q + 128], in_=src, func=ACT.Copy, scale=sc)
+
+        def turn(u):
+            tp = psum.tile([P, 2, 2, P], F32, name="tp")
+            tps[u] = tp
+            for a in range(2):
+                w = wide[u][:, a, :].bitcast(F32)
+                for i in range(2):
+                    cols = slice(128 * i, 128 * i + 128) if ON_VECTOR[u] else slice(i, 256, 2)
+                    nc.tensor.transpose(tp[:, a, i, :], w[:, cols], ident[:])
+
+        def empty(u):
+            gr = work.tile([P, 1024], BF16, name="grouped", bufs=6, align_bytes=64)
+            grouped[u] = gr
+            nc.scalar.copy(
+                out=gr[:].bitcast(F32).rearrange("p (a m u) -> p a m u", a=2, u=2),
+                in_=tps[u][:].rearrange("p a u m -> p a m u"),
+            )
+
+        def quant(u):
+            j, g = u // 3, u % 3
+            nc.vector.quantize_mx(
+                out=codes[j][:, g, :].bitcast(FP8X4), scales=scales[j][:, g, :], in_=grouped[u][:]
+            )
+
+        def passes_h(bank, slot, j, s):
+            a = slot % 2
+            for g in range(NG):
+                nc.tensor.matmul_mx(
+                    out=bank[:, slot, :],
+                    lhsT=codes[j][:, g, 128 * a : 128 * a + 128].bitcast(FP8X4),
+                    lhsT_scale=scales[j][:, g, 128 * a : 128 * a + 128],
+                    rhs=words[s // 4][:, g, 256 * (s % 4) : 256 * (s % 4) + 256].bitcast(FP4X4),
+                    rhs_scale=cvs[:, g, 128 * s : 128 * s + 128],
+                    start=(g == 0),
+                    stop=(g == NG - 1),
+                )
+
+        def left(j):
+            for s in range(4):
+                if j % 2 == 0:
+                    bank = psum.tile([P, 4, P], F32, name=f"h{s}", bufs=1)
+                    hb[j // 2, s] = bank
+                for a in range(2):
+                    passes_h(hb[j // 2, s], 2 * (j % 2) + a, j, s)
+
+        def right(k):
+            h, s = k % 6 // 2, 4 + 2 * (k // 6) + k % 2
+            bank = psum.tile([P, 4, P], F32, name=f"h{k % 4}", bufs=1)
+            hb[h, s] = bank
+            for slot in range(4):
+                passes_h(bank, slot, 2 * h + slot // 2, s)
+
+        def add_l(h, s):
+            if s % 2 == 0:
+                hi[h, s // 2] = work.tile([P, 256, 4], BF16, name="hi", align_bytes=64)
+            c = 128 * (s % 2)
+            lc = 128 * (s % 4)
+            nc.vector.tensor_tensor(
+                out=hi[h, s // 2][:, c : c + 128, :],
+                in0=hb[h, s][:].rearrange("p t n -> p n t"),
+                in1=lt[h][s // 4][:, :, lc : lc + 128].rearrange("p t n -> p n t"),
+                op=ADD,
+            )
+
+        def quant_h(h, sp):
+            v, c = sp // 2, 256 * (sp % 2)
+            nc.vector.quantize_mx(
+                out=hc[v][:, h, c : c + 256].bitcast(FP8X4),
+                scales=hs[v][:, h, c : c + 256],
+                in_=hi[h, sp][:].rearrange("p n t -> p (n t)"),
+            )
+
+        def right_add(k):
+            h, s = k % 6 // 2, 4 + 2 * (k // 6) + k % 2
+            add_l(h, s)
+            if s % 2 == 1:
+                quant_h(h, s // 2)
+
+        def product(r, n0, n):
+            f = psum.tile([P, n], F32, name="tp")
+            v, c, a = n0 // 512, n0 % 512, r % 2
+            for h in range(NG):
+                nc.tensor.matmul_mx(
+                    out=f[:],
+                    lhsT=codes[6 + r // 2][:, h, 128 * a : 128 * a + 128].bitcast(FP8X4),
+                    lhsT_scale=scales[6 + r // 2][:, h, 128 * a : 128 * a + 128],
+                    rhs=hc[v][:, h, c : c + n].bitcast(FP8X4),
+                    rhs_scale=hs[v][:, h, c : c + n],
+                    start=(h == 0),
+                    stop=(h == NG - 1),
+                )
+            cols = slice(n0, n0 + n)
+            fo = work.tile([P, n], F32, name="fo", bufs=8)
+            nc.scalar.copy(out=fo[:], in_=f[:])
+            nc.sync.dma_start(out=fv[:, r, cols], in_=fo[:])
+            mo = work.tile([P, n], F32, name="mo", bufs=8)
+            nc.vector.scalar_tensor_tensor(
+                out=mo[:], in0=f[:], scalar=-1.0, in1=rec[r][:, cols], op0=MULT, op1=MULT
+            )
+            nc.sync.dma_start(out=mv[:, r, cols], in_=mo[:])
+
+        def ln(r):
+            nc.scalar.activation(out=rec[r][:], in_=ev[:], func=ACT.Ln, bias=neo[:, r : r + 1])
+
+        todo = {}
+        for h in range(NG):
+            first = 6 * h + 5 + MOFF
+            for d, what, s in ADDS:
+                todo.setdefault(first + d, []).append((what, h, s))
+        names = {"a": add_l, "q": quant_h}
+
+        for u in range(AHEAD):
+            widen(u)
+            if u < 3:
+                turn(u)
+        k_made = 0
+        k_added = 0
+        n_ln = 0
+        for u in range(24 + max(QLAG, MOFF)):
+            if QFIRST and 0 <= u - QLAG < 24:
+                quant(u - QLAG)
+            if u < 24:
+                empty(u)
+            if u + AHEAD < 24:
+                widen(u + AHEAD)
+            if u % 3 == TOFF and u // 3 < 7:
+                for i in range(3):
+                    turn(u // 3 * 3 + 3 + i)
+            for what, h, s in todo.get(u, []):
+                names[what](h, s)
+            if not QFIRST and 0 <= u - QLAG < 24:
+                quant(u - QLAG)
+            if k_added < k_made and k_added < 6:
+                right_add(k_added)
+                k_added += 1
+            if u == 18:
+                nc.vector.tensor_scalar(out=neo[:], in0=eo[:], scalar1=-1.0, scalar2=None, op0=MULT)
+            if u > LN0 and n_ln < 4:
+                ln(n_ln)
+                n_ln += 1
+            if u >= 2 + MOFF and (u - MOFF) % 3 == 2 and (u - MOFF) // 3 < 6:
+                left((u - MOFF) // 3)
+            if u >= 18 + MOFF - RB and k_made < 6:
+                right(k_made)
+                k_made += 1
+        while k_made < 6:
+            right(k_made)
+            k_made += 1
+        while k_added < 6:
+            right_add(k_added)
+            k_added += 1
+        for r in range(4):
+            nc.scalar.activation(out=rec[r][:], in_=rec[r][:], func=ACT.Exp, scale=-1.0)
+            product(r, 0, 512)
+            right(6 + r)
+            right_add(6 + r)
+        for k in (10, 11):
+            right(k)
+            right_add(k)
+        for n0 in (512, 768):
+            for r in range(4):
+                product(r, n0, 256)

@@ -22,14 +22,15 @@ ACT = mybir.ActivationFunctionType
 
 NG = 3
 AHEAD = 5
-QLAG = 1
-QFIRST = True
-TOFF = 2
+LORDER = "g"
+QLAG = 0
+QFIRST = False
+TOFF = 1
 MOFF = 1
-RB = 0
-LN0 = 18
-ADDS = [(1, "a", 0), (2, "a", 1), (2, "a", 2), (3, "a", 3), (3, "q", 0), (4, "q", 1)]
-ON_VECTOR = [u % 2 == 0 for u in range(24)]
+RB = -1
+LN0 = 20
+ADDS = [(1, "a", 0), (1, "a", 1), (2, "a", 2), (2, "a", 3), (3, "q", 0), (4, "q", 1)]
+ON_VECTOR = [u in (1, 3, 4, 5, 6, 8, 9, 10, 12, 14, 16, 18, 20, 22, 23) for u in range(24)]
 
 
 def tile_fock_orbital_transform_d6_kernel(
@@ -73,13 +74,13 @@ def tile_fock_orbital_transform_d6_kernel(
         make_identity(nc, ident[:])
         nc.scalar.dma_start(out=gs[:], in_=G_scale.rearrange("(h p t) b -> p h t b", p=P, t=4))
         nc.scalar.activation(out=dummy[:], in_=dummy[:], func=ACT.Ln)
-        nc.sync.dma_start(out=gb[0][:, 0, :], in_=gv[0][:, 0, :])
-        nc.sync.dma_start(out=gb[0][:, 1, :], in_=gv[0][:, 1, :])
+        nc.sync.dma_start(out=gb[0][:, :, 0:512], in_=gv[0][:, 0:2, 0:512])
+        nc.sync.dma_start(out=gb[0][:, :, 512:A], in_=gv[0][:, 0:2, 512:A])
+        nc.sync.dma_start(out=gb[1][:], in_=gv[0][:, 2:4, :])
         for q in range(4):
             nc.scalar.dma_start(
                 out=cvs[:].bitcast(I32)[32 * q : 32 * q + 4], in_=sv[4 * q : 4 * q + 4]
             )
-        nc.sync.dma_start(out=gb[1][:], in_=gv[0][:, 2:4, :])
         nc.sync.dma_start(out=words[0][:].bitcast(I32), in_=wv[:, :, 0:256])
         nc.sync.dma_start(out=gb[2][:], in_=gv[1][:, 0:2, :])
         nc.sync.dma_start(out=lt[0][0][:], in_=lv[0][:, :, 0:512])
@@ -147,33 +148,42 @@ def tile_fock_orbital_transform_d6_kernel(
                 out=codes[j][:, g, :].bitcast(FP8X4), scales=scales[j][:, g, :], in_=grouped[u][:]
             )
 
-        def passes_h(bank, slot, j, s):
+        def one_pass(bank, slot, j, s, g):
             a = slot % 2
-            for g in range(NG):
-                nc.tensor.matmul_mx(
-                    out=bank[:, slot, :],
-                    lhsT=codes[j][:, g, 128 * a : 128 * a + 128].bitcast(FP8X4),
-                    lhsT_scale=scales[j][:, g, 128 * a : 128 * a + 128],
-                    rhs=words[s // 4][:, g, 256 * (s % 4) : 256 * (s % 4) + 256].bitcast(FP4X4),
-                    rhs_scale=cvs[:, g, 128 * s : 128 * s + 128],
-                    start=(g == 0),
-                    stop=(g == NG - 1),
-                )
+            nc.tensor.matmul_mx(
+                out=bank[:, slot, :],
+                lhsT=codes[j][:, g, 128 * a : 128 * a + 128].bitcast(FP8X4),
+                lhsT_scale=scales[j][:, g, 128 * a : 128 * a + 128],
+                rhs=words[s // 4][:, g, 256 * (s % 4) : 256 * (s % 4) + 256].bitcast(FP4X4),
+                rhs_scale=cvs[:, g, 128 * s : 128 * s + 128],
+                start=(g == 0),
+                stop=(g == NG - 1),
+            )
 
         def left(j):
-            for s in range(4):
-                if j % 2 == 0:
+            slot = 2 * (j % 2)
+            if j % 2 == 0:
+                for s in range(4):
                     bank = psum.tile([P, 4, P], F32, name=f"h{s}", bufs=1)
                     hb[j // 2, s] = bank
-                for a in range(2):
-                    passes_h(hb[j // 2, s], 2 * (j % 2) + a, j, s)
+            for x in range(12):
+                s, g = (x % 4, x // 4) if LORDER == "g" else (x // 3, x % 3)
+                one_pass(hb[j // 2, s], slot, j, s, g)
+                if LORDER == "s" and g == 2:
+                    for gg in range(NG):
+                        one_pass(hb[j // 2, s], slot + 1, j, s, gg)
+            if LORDER == "g":
+                for s in range(4):
+                    for g in range(NG):
+                        one_pass(hb[j // 2, s], slot + 1, j, s, g)
 
         def right(k):
             h, s = k % 6 // 2, 4 + 2 * (k // 6) + k % 2
             bank = psum.tile([P, 4, P], F32, name=f"h{k % 4}", bufs=1)
             hb[h, s] = bank
             for slot in range(4):
-                passes_h(bank, slot, 2 * h + slot // 2, s)
+                for g in range(NG):
+                    one_pass(bank, slot, 2 * h + slot // 2, s, g)
 
         def add_l(h, s):
             if s % 2 == 0:
@@ -181,9 +191,9 @@ def tile_fock_orbital_transform_d6_kernel(
             c = 128 * (s % 2)
             lc = 128 * (s % 4)
             nc.vector.tensor_tensor(
-                out=hi[h, s // 2][:, c : c + 128, :],
-                in0=hb[h, s][:].rearrange("p t n -> p n t"),
-                in1=lt[h][s // 4][:, :, lc : lc + 128].rearrange("p t n -> p n t"),
+                out=hi[h, s // 2][:, c : c + 128, :].rearrange("p (c i) t -> p c t i", i=4),
+                in0=hb[h, s][:].rearrange("p t (c i) -> p c t i", i=4),
+                in1=lt[h][s // 4][:, :, lc : lc + 128].rearrange("p t (c i) -> p c t i", i=4),
                 op=ADD,
             )
 
@@ -201,6 +211,8 @@ def tile_fock_orbital_transform_d6_kernel(
             if s % 2 == 1:
                 quant_h(h, s // 2)
 
+        outs = {}
+
         def product(r, n0, n):
             f = psum.tile([P, n], F32, name="tp")
             v, c, a = n0 // 512, n0 % 512, r % 2
@@ -215,14 +227,20 @@ def tile_fock_orbital_transform_d6_kernel(
                     stop=(h == NG - 1),
                 )
             cols = slice(n0, n0 + n)
-            fo = work.tile([P, n], F32, name="fo", bufs=8)
-            nc.scalar.copy(out=fo[:], in_=f[:])
-            nc.sync.dma_start(out=fv[:, r, cols], in_=fo[:])
-            mo = work.tile([P, n], F32, name="mo", bufs=8)
+            m = 512 // n
+            i = r % m
+            if i == 0:
+                fo = work.tile([P, m, n], F32, name="fo", bufs=8)
+                mo = work.tile([P, m, n], F32, name="mo", bufs=8)
+                outs[0] = (fo, mo)
+            fo, mo = outs[0]
+            nc.scalar.copy(out=fo[:, i, :], in_=f[:])
             nc.vector.scalar_tensor_tensor(
-                out=mo[:], in0=f[:], scalar=-1.0, in1=rec[r][:, cols], op0=MULT, op1=MULT
+                out=mo[:, i, :], in0=f[:], scalar=-1.0, in1=rec[r][:, cols], op0=MULT, op1=MULT
             )
-            nc.sync.dma_start(out=mv[:, r, cols], in_=mo[:])
+            if i == m - 1:
+                nc.sync.dma_start(out=fv[:, r - i : r + 1, cols], in_=fo[:])
+                nc.sync.dma_start(out=mv[:, r - i : r + 1, cols], in_=mo[:])
 
         def ln(r):
             nc.scalar.activation(out=rec[r][:], in_=ev[:], func=ACT.Ln, bias=neo[:, r : r + 1])
@@ -282,6 +300,9 @@ def tile_fock_orbital_transform_d6_kernel(
         for k in (10, 11):
             right(k)
             right_add(k)
-        for n0 in (512, 768):
-            for r in range(4):
-                product(r, n0, 256)
+            if k == 10:
+                product(0, 512, 256)
+        for r in range(1, 4):
+            product(r, 512, 256)
+        for r in range(4):
+            product(r, 768, 256)

@@ -22,15 +22,17 @@ ACT = mybir.ActivationFunctionType
 
 NG = 3
 AHEAD = 5
+WARM0 = 8
+WARM = {5: 2, 9: 1}
 LORDER = "g"
-QLAG = 0
-QFIRST = False
-TOFF = 1
-MOFF = 1
-RB = -1
-LN0 = 20
-ADDS = [(1, "a", 0), (1, "a", 1), (2, "a", 2), (2, "a", 3), (3, "q", 0), (4, "q", 1)]
-ON_VECTOR = [u in (1, 3, 4, 5, 6, 8, 9, 10, 12, 14, 16, 18, 20, 22, 23) for u in range(24)]
+QLAG = 1
+QFIRST = True
+TOFF = 2
+MOFF = 2
+RB = 0
+LN0 = 18
+ADDS = [(1, "a", 0), (1, "a", 1), (1, "a", 2), (1, "a", 3), (3, "q", 0), (4, "q", 1)]
+ON_VECTOR = [u in (0, 1, 3, 4, 5, 6, 8, 9, 11, 12, 14, 16, 17, 20, 22, 23) for u in range(24)]
 
 
 def tile_fock_orbital_transform_d6_kernel(
@@ -58,6 +60,7 @@ def tile_fock_orbital_transform_d6_kernel(
         hc = [keep.tile([P, NG, 512], U32, name=f"hc{v}", align_bytes=64) for v in range(2)]
         hs = [keep.tile([P, NG, 512], U8, name=f"hs{v}", align_bytes=64) for v in range(2)]
         rec = [keep.tile([P, V], F32, name=f"rec{r}") for r in range(4)]
+        zeros = keep.tile([P, 512], BF16, name="zeros", align_bytes=64)
         neo = keep.tile([P, 4], F32, name="neo")
         dummy = keep.tile([P, 1], F32, name="dummy")
 
@@ -69,6 +72,7 @@ def tile_fock_orbital_transform_d6_kernel(
         fv = out_0.rearrange("(p r) n -> p r n", r=4)
         mv = out_1.rearrange("(p r) n -> p r n", r=4)
 
+        nc.vector.memset(zeros[:], 0.0)
         nc.vector.memset(dummy[:], 1.0)
         nc.gpsimd.memset(cvs[:].bitcast(I32), 0)
         make_identity(nc, ident[:])
@@ -105,6 +109,13 @@ def tile_fock_orbital_transform_d6_kernel(
         hb = {}
         hi = {}
 
+        def warm(bank):
+            nc.tensor.matmul(out=bank, lhsT=zeros[:, 0:P], rhs=zeros[:], start=True, stop=True)
+
+        wb = psum.tile([P, 512], F32, name="h0", bufs=1)
+        for _ in range(WARM0):
+            warm(wb[:])
+
         def widen(u):
             j, g = u // 3, u % 3
             w = work.tile([P, 2, 512], BF16, name="wide", bufs=8, align_bytes=64)
@@ -128,6 +139,8 @@ def tile_fock_orbital_transform_d6_kernel(
         def turn(u):
             tp = psum.tile([P, 2, 2, P], F32, name="tp")
             tps[u] = tp
+            for _ in range(WARM.get(u, 0)):
+                warm(tp[:].rearrange("p a u m -> p (a u m)"))
             for a in range(2):
                 w = wide[u][:, a, :].bitcast(F32)
                 for i in range(2):

from contextlib import ExitStack

import concourse.mybir as mybir
from concourse.masks import make_identity

FLOPS = 2 * 1536 * 1536 * 1024 + 2 * 512 * 1536 * 1024

A, O, V = 1536, 512, 1024
P = 128

F32 = mybir.dt.float32
BF16 = mybir.dt.bfloat16
I32 = mybir.dt.int32
U32 = mybir.dt.uint32
U8 = mybir.dt.uint8
FP8 = mybir.dt.float8_e4m3fn
FP8X4 = mybir.dt.float8_e4m3fn_x4
FP4X4 = mybir.dt.float4_e2m1fn_x4
MULT = mybir.AluOpType.mult
ADD = mybir.AluOpType.add
ACT = mybir.ActivationFunctionType

NG = 3
AHEAD = 5
WARM0 = 8
WARM = {5: 2, 9: 1}
LORDER = "g"
QLAG = 1
QFIRST = True
TOFF = 2
MOFF = 2
RB = 0
LN0 = 18
ADDS = [(1, "a", 0), (1, "a", 1), (1, "a", 2), (1, "a", 3), (3, "q", 0), (4, "q", 1)]
ON_VECTOR = [u in (0, 1, 3, 4, 5, 6, 8, 9, 11, 12, 14, 16, 17, 20, 22, 23) for u in range(24)]


def tile_fock_orbital_transform_d6_kernel(
    tc, G_bytes, G_scale, Cv_words, Cv_scales, L, Co_bytes, Co_scale, e_o, e_v, out_0, out_1
):
    nc = tc.nc
    with ExitStack() as ctx:
        keep = ctx.enter_context(tc.tile_pool(name="keep", bufs=1))
        work = ctx.enter_context(tc.tile_pool(name="work", bufs=3))
        psum = ctx.enter_context(tc.psum_pool(name="psum", bufs=4))
        ctx.enter_context(tc.manual_schedule())

        ident = keep.tile([P, P], F32, name="ident")
        gs = keep.tile([P, NG, 4, 12], F32, name="gs")
        cos = keep.tile([P, 12], F32, name="cos")
        gb = [keep.tile([P, 2, A], U8, name=f"gb{j}", align_bytes=64) for j in range(6)]
        cb = [keep.tile([P, 2, A], U8, name=f"cb{j}", align_bytes=64) for j in range(2)]
        words = [keep.tile([P, NG, 1024], U8, name=f"words{v}", align_bytes=64) for v in range(2)]
        cvs = keep.tile([P, NG, V], U8, name="cvs", align_bytes=64)
        lt = [[keep.tile([P, 4, 512], BF16, name=f"lt{h}_{v}", align_bytes=64) for v in range(2)] for h in range(NG)]
        eo = keep.tile([P, 4], BF16, name="eo")
        ev = keep.tile([P, V], BF16, name="ev")
        codes = [keep.tile([P, NG, 256], U32, name=f"codes{j}", align_bytes=64) for j in range(8)]
        scales = [keep.tile([P, NG, 256], U8, name=f"scales{j}", align_bytes=64) for j in range(8)]
        hc = [keep.tile([P, NG, 512], U32, name=f"hc{v}", align_bytes=64) for v in range(2)]
        hs = [keep.tile([P, NG, 512], U8, name=f"hs{v}", align_bytes=64) for v in range(2)]
        rec = [keep.tile([P, V], F32, name=f"rec{r}") for r in range(4)]
        zeros = keep.tile([P, 512], BF16, name="zeros", align_bytes=64)
        neo = keep.tile([P, 4], F32, name="neo")
        dummy = keep.tile([P, 1], F32, name="dummy")

        gv = G_bytes.rearrange("(h p t) k -> h p t k", p=P, t=4)
        cv = Co_bytes.rearrange("(p r) k -> p r k", r=4)
        lv = L.rearrange("(h p t) n -> h p t n", p=P, t=4)
        wv = Cv_words.bitcast(I32).rearrange("g p w -> p g w")
        sv = Cv_scales.bitcast(I32).rearrange("g q w -> q g w")
        fv = out_0.rearrange("(p r) n -> p r n", r=4)
        mv = out_1.rearrange("(p r) n -> p r n", r=4)

        nc.vector.memset(zeros[:], 0.0)
        nc.vector.memset(dummy[:], 1.0)
        nc.gpsimd.memset(cvs[:].bitcast(I32), 0)
        make_identity(nc, ident[:])
        nc.scalar.dma_start(out=gs[:], in_=G_scale.rearrange("(h p t) b -> p h t b", p=P, t=4))
        nc.scalar.activation(out=dummy[:], in_=dummy[:], func=ACT.Ln)
        nc.sync.dma_start(out=gb[0][:, :, 0:512], in_=gv[0][:, 0:2, 0:512])
        nc.sync.dma_start(out=gb[0][:, :, 512:A], in_=gv[0][:, 0:2, 512:A])
        nc.sync.dma_start(out=gb[1][:], in_=gv[0][:, 2:4, :])
        for q in range(4):
            nc.scalar.dma_start(
                out=cvs[:].bitcast(I32)[32 * q : 32 * q + 4], in_=sv[4 * q : 4 * q + 4]
            )
        nc.sync.dma_start(out=words[0][:].bitcast(I32), in_=wv[:, :, 0:256])
        nc.sync.dma_start(out=gb[2][:], in_=gv[1][:, 0:2, :])
        nc.sync.dma_start(out=lt[0][0][:], in_=lv[0][:, :, 0:512])
        nc.sync.dma_start(out=gb[3][:], in_=gv[1][:, 2:4, :])
        nc.sync.dma_start(out=gb[4][:], in_=gv[2][:, 0:2, :])
        nc.sync.dma_start(out=lt[1][0][:], in_=lv[1][:, :, 0:512])
        nc.sync.dma_start(out=gb[5][:], in_=gv[2][:, 2:4, :])
        for c in range(4):
            nc.sync.dma_start(out=cos[32 * c : 32 * c + 32], in_=Co_scale[c].partition_broadcast(32))
        nc.sync.dma_start(out=cb[0][:], in_=cv[:, 0:2, :])
        nc.sync.dma_start(out=lt[2][0][:], in_=lv[2][:, :, 0:512])
        nc.sync.dma_start(out=cb[1][:], in_=cv[:, 2:4, :])
        nc.sync.dma_start(out=words[1][:].bitcast(I32), in_=wv[:, :, 256:512])
        nc.sync.dma_start(out=eo[:], in_=e_o.rearrange("(p r) -> p r", r=4))
        for h in range(NG):
            nc.sync.dma_start(out=lt[h][1][:], in_=lv[h][:, :, 512:1024])
        nc.sync.dma_start(out=ev[:], in_=e_v.partition_broadcast(P))

        wide = {}
        tps = {}
        grouped = {}
        hb = {}
        hi = {}

        def warm(bank):
            nc.tensor.matmul(out=bank, lhsT=zeros[:, 0:P], rhs=zeros[:], start=True, stop=True)

        wb = psum.tile([P, 512], F32, name="h0", bufs=1)
        for _ in range(WARM0):
            warm(wb[:])

        def widen(u):
            j, g = u // 3, u % 3
            w = work.tile([P, 2, 512], BF16, name="wide", bufs=8, align_bytes=64)
            wide[u] = w
            for q in range(4):
                b = 4 * g + q
                for a in range(2):
                    src = (gb[j] if j < 6 else cb[j - 6])[:, a, 128 * b : 128 * b + 128].bitcast(FP8)
                    sc = gs[:, j // 2, 2 * (j % 2) + a, b : b + 1] if j < 6 else cos[:, b : b + 1]
                    if ON_VECTOR[u]:
                        nc.vector.tensor_scalar(
                            out=w[:, a, :].rearrange("p (u x e) -> p x u e", u=2, e=2)[:, 32 * q : 32 * q + 32],
                            in0=src.rearrange("p (x u e) -> p x u e", u=2, e=2),
                            scalar1=sc,
                            scalar2=None,
                            op0=MULT,
                        )
                    else:
                        nc.scalar.activation(out=w[:, a, 128 * q : 128 * q + 128], in_=src, func=ACT.Copy, scale=sc)

        def turn(u):
            tp = psum.tile([P, 2, 2, P], F32, name="tp")
            tps[u] = tp
            for _ in range(WARM.get(u, 0)):
                warm(tp[:].rearrange("p a u m -> p (a u m)"))
            for a in range(2):
                w = wide[u][:, a, :].bitcast(F32)
                for i in range(2):
                    cols = slice(128 * i, 128 * i + 128) if ON_VECTOR[u] else slice(i, 256, 2)
                    nc.tensor.transpose(tp[:, a, i, :], w[:, cols], ident[:])

        def empty(u):
            gr = work.tile([P, 1024], BF16, name="grouped", bufs=6, align_bytes=64)
            grouped[u] = gr
            nc.scalar.copy(
                out=gr[:].bitcast(F32).rearrange("p (a m u) -> p a m u", a=2, u=2),
                in_=tps[u][:].rearrange("p a u m -> p a m u"),
            )

        def quant(u):
            j, g = u // 3, u % 3
            nc.vector.quantize_mx(
                out=codes[j][:, g, :].bitcast(FP8X4), scales=scales[j][:, g, :], in_=grouped[u][:]
            )

        def one_pass(bank, slot, j, s, g):
            a = slot % 2
            nc.tensor.matmul_mx(
                out=bank[:, slot, :],
                lhsT=codes[j][:, g, 128 * a : 128 * a + 128].bitcast(FP8X4),
                lhsT_scale=scales[j][:, g, 128 * a : 128 * a + 128],
                rhs=words[s // 4][:, g, 256 * (s % 4) : 256 * (s % 4) + 256].bitcast(FP4X4),
                rhs_scale=cvs[:, g, 128 * s : 128 * s + 128],
                start=(g == 0),
                stop=(g == NG - 1),
            )

        def left(j):
            slot = 2 * (j % 2)
            if j % 2 == 0:
                for s in range(4):
                    bank = psum.tile([P, 4, P], F32, name=f"h{s}", bufs=1)
                    hb[j // 2, s] = bank
            for x in range(12):
                s, g = (x % 4, x // 4) if LORDER == "g" else (x // 3, x % 3)
                one_pass(hb[j // 2, s], slot, j, s, g)
                if LORDER == "s" and g == 2:
                    for gg in range(NG):
                        one_pass(hb[j // 2, s], slot + 1, j, s, gg)
            if LORDER == "g":
                for s in range(4):
                    for g in range(NG):
                        one_pass(hb[j // 2, s], slot + 1, j, s, g)

        def right(k):
            h, s = k % 6 // 2, 4 + 2 * (k // 6) + k % 2
            bank = psum.tile([P, 4, P], F32, name=f"h{k % 4}", bufs=1)
            hb[h, s] = bank
            for slot in range(4):
                for g in range(NG):
                    one_pass(bank, slot, 2 * h + slot // 2, s, g)

        def add_l(h, s):
            if s % 2 == 0:
                hi[h, s // 2] = work.tile([P, 256, 4], BF16, name="hi", align_bytes=64)
            c = 128 * (s % 2)
            lc = 128 * (s % 4)
            nc.vector.tensor_tensor(
                out=hi[h, s // 2][:, c : c + 128, :].rearrange("p (c i) t -> p c t i", i=4),
                in0=hb[h, s][:].rearrange("p t (c i) -> p c t i", i=4),
                in1=lt[h][s // 4][:, :, lc : lc + 128].rearrange("p t (c i) -> p c t i", i=4),
                op=ADD,
            )

        def quant_h(h, sp):
            v, c = sp // 2, 256 * (sp % 2)
            nc.vector.quantize_mx(
                out=hc[v][:, h, c : c + 256].bitcast(FP8X4),
                scales=hs[v][:, h, c : c + 256],
                in_=hi[h, sp][:].rearrange("p n t -> p (n t)"),
            )

        def right_add(k):
            h, s = k % 6 // 2, 4 + 2 * (k // 6) + k % 2
            add_l(h, s)
            if s % 2 == 1:
                quant_h(h, s // 2)

        outs = {}

        def product(r, n0, n):
            f = psum.tile([P, n], F32, name="tp")
            v, c, a = n0 // 512, n0 % 512, r % 2
            for h in range(NG):
                nc.tensor.matmul_mx(
                    out=f[:],
                    lhsT=codes[6 + r // 2][:, h, 128 * a : 128 * a + 128].bitcast(FP8X4),
                    lhsT_scale=scales[6 + r // 2][:, h, 128 * a : 128 * a + 128],
                    rhs=hc[v][:, h, c : c + n].bitcast(FP8X4),
                    rhs_scale=hs[v][:, h, c : c + n],
                    start=(h == 0),
                    stop=(h == NG - 1),
                )
            cols = slice(n0, n0 + n)
            m = 512 // n
            i = r % m
            if i == 0:
                fo = work.tile([P, m, n], F32, name="fo", bufs=8)
                mo = work.tile([P, m, n], F32, name="mo", bufs=8)
                outs[0] = (fo, mo)
            fo, mo = outs[0]
            nc.scalar.copy(out=fo[:, i, :], in_=f[:])
            nc.vector.scalar_tensor_tensor(
                out=mo[:, i, :], in0=f[:], scalar=-1.0, in1=rec[r][:, cols], op0=MULT, op1=MULT
            )
            if i == m - 1:
                nc.sync.dma_start(out=fv[:, r - i : r + 1, cols], in_=fo[:])
                nc.sync.dma_start(out=mv[:, r - i : r + 1, cols], in_=mo[:])

        def ln(r):
            nc.scalar.activation(out=rec[r][:], in_=ev[:], func=ACT.Ln, bias=neo[:, r : r + 1])

        todo = {}
        for h in range(NG):
            first = 6 * h + 5 + MOFF
            for d, what, s in ADDS:
                todo.setdefault(first + d, []).append((what, h, s))
        names = {"a": add_l, "q": quant_h}

        for u in range(AHEAD):
            widen(u)
            if u < 3:
                turn(u)
        k_made = 0
        k_added = 0
        n_ln = 0
        for u in range(24 + max(QLAG, MOFF)):
            if QFIRST and 0 <= u - QLAG < 24:
                quant(u - QLAG)
            if u < 24:
                empty(u)
            if u + AHEAD < 24:
                widen(u + AHEAD)
            if u % 3 == TOFF and u // 3 < 7:
                for i in range(3):
                    turn(u // 3 * 3 + 3 + i)
            for what, h, s in todo.get(u, []):
                names[what](h, s)
            if not QFIRST and 0 <= u - QLAG < 24:
                quant(u - QLAG)
            if k_added < k_made and k_added < 6:
                right_add(k_added)
                k_added += 1
            if u == 18:
                nc.vector.tensor_scalar(out=neo[:], in0=eo[:], scalar1=-1.0, scalar2=None, op0=MULT)
            if u > LN0 and n_ln < 4:
                ln(n_ln)
                n_ln += 1
            if u >= 2 + MOFF and (u - MOFF) % 3 == 2 and (u - MOFF) // 3 < 6:
                left((u - MOFF) // 3)
            if u >= 18 + MOFF - RB and k_made < 6:
                right(k_made)
                k_made += 1
        while k_made < 6:
            right(k_made)
            k_made += 1
        while k_added < 6:
            right_add(k_added)
            k_added += 1
        for r in range(4):
            nc.scalar.activation(out=rec[r][:], in_=rec[r][:], func=ACT.Exp, scale=-1.0)
            product(r, 0, 512)
            right(6 + r)
            right_add(6 + r)
        for k in (10, 11):
            right(k)
            right_add(k)
            if k == 10:
                product(0, 512, 256)
        for r in range(1, 4):
            product(r, 512, 256)
        for r in range(4):
            product(r, 768, 256)
